import numpy as np
import ml_dtypes


def mxq(x, axis, fmt="e4m3"):
    dtype, down = {"e4m3": (ml_dtypes.float8_e4m3fn, 7), "e5m2": (ml_dtypes.float8_e5m2, 14)}[fmt]
    v = np.moveaxis(np.asarray(x, np.float32).astype(ml_dtypes.bfloat16).astype(np.float64), axis, -1)
    blocks = v.reshape(v.shape[:-1] + (-1, 32))
    amax = np.abs(blocks).max(-1, keepdims=True)
    byte = np.maximum(np.where(amax > 0, np.frexp(amax)[1] - 1 + 127, 0) - down, 1)
    scale = np.exp2(byte - 127.0)
    codes = (blocks / scale).astype(np.float32).astype(dtype).astype(np.float64)
    return np.moveaxis((codes * scale).reshape(v.shape), -1, axis)


WIDE = False


def mx_kscale(k):
    if not WIDE:
        return np.ones(k)
    levels = np.array([10, -10, 5, -5, 0])
    if k % 512:
        return np.exp2(np.random.permutation(np.resize(levels, k // 32))).repeat(32)
    a = np.empty((k // 512, 16))
    for p in range(k // 512):
        a[p, :8] = np.random.permutation(np.resize(levels, 8))
        for g in range(8):
            far = levels[np.abs(levels - a[p, g]) >= 10]
            a[p, g + 8] = far[np.random.randint(len(far))]
    return np.exp2(a.ravel()).repeat(32)


def f64(x):
    return np.asarray(x).astype(np.float64)


def striped8(idx):
    return np.asarray(idx).reshape(8, -1, 16).transpose(0, 2, 1).reshape(128, -1).astype(np.uint16)


def unstriped8(offs):
    return offs.reshape(8, 16, -1).transpose(0, 2, 1).reshape(8, -1).astype(np.int64)


def pick8(x, idx, run):
    r = np.arange(len(x))
    return x[r[:, None], idx[r % (8 * run) // run]]


E2M1 = np.array([0.0, 0.5, 1.0, 1.5, 2.0, 3.0, 4.0, 6.0, -0.0, -0.5, -1.0, -1.5, -2.0, -3.0, -4.0, -6.0])


def pack_weight(w, fmt):
    k, n = w.shape
    w = f64(np.asarray(w, np.float32).astype(ml_dtypes.bfloat16)).reshape(k // 32, 32, n)
    amax = np.abs(w).max(1)
    if fmt == "e4m3":
        byte = np.frexp(amax)[1] - 1 + 127 - 7
    else:
        mant, ex = np.frexp(amax / 6.0)
        byte = np.where(mant > 0.5, ex, ex - 1) + 127
    byte = np.clip(np.where(amax > 0, byte, 1), 1, 254)
    scaled = (w * np.exp2(127.0 - byte)[:, None, :]).reshape(k, n).astype(np.float32)
    by_word = np.ascontiguousarray(scaled.reshape(k // 512, 128, 4, n).transpose(0, 1, 3, 2))
    if fmt == "e4m3":
        words = by_word.astype(ml_dtypes.float8_e4m3fn).view(np.uint8)
    else:
        c = by_word.astype(ml_dtypes.float4_e2m1fn).view(np.uint8) & 0xF
        words = (c[..., 0::2] | (c[..., 1::2] << 4)).reshape(k // 512, 128, 2 * n)
    return np.ascontiguousarray(words), np.ascontiguousarray(byte.astype(np.uint8).reshape(k // 512, 16, n))


def unpack_weight(words, scales, fmt):
    g, _, n = scales.shape
    words = np.ascontiguousarray(words).reshape(g, 128, n, -1)
    if fmt == "e4m3":
        vals = words.view(ml_dtypes.float8_e4m3fn).astype(np.float64)
    else:
        nib = np.empty((g, 128, n, 4), np.uint8)
        nib[..., 0::2] = words & 0xF
        nib[..., 1::2] = words >> 4
        vals = E2M1[nib]
    vals = vals * np.repeat(np.exp2(scales.astype(np.float64) - 127.0), 8, axis=1)[..., None]
    return vals.transpose(0, 1, 3, 2).reshape(g * 512, n)


D, E, T, Q, I = 512, 512, 1024, 128, 512


def setup_inputs():
    n = np.random.standard_normal
    idx = np.stack([np.random.permutation(T)[:I] for _ in range(8)])
    idx2 = np.stack([np.random.permutation(T)[:I] for _ in range(8)])
    fd = mx_kscale(D)
    fe = mx_kscale(E)
    keysp = pack_weight(n((D, T)) / fd[:, None], "e2m1")
    return {
        "query": (n((D, Q)) * 0.6 / np.sqrt(D) * fd[:, None]).astype(np.float32),
        "keys_words": keysp[0],
        "keys_scales": keysp[1],
        "gout": (n((E, Q)) * 1 / np.sqrt(E) * fe[:, None]).astype(np.float32),
        "vals": (n((E, T)) / fe[:, None]).astype(np.float32),
        "share": (np.random.uniform(0.4, 0.9, (Q, 1))).astype(np.float32),
        "fac": (np.random.uniform(0.5, 2.0, (1, T))).astype(np.float32),
        "old": (0.5 * n((Q, T))).astype(np.float32),
        "offs": striped8(idx),
        "offs2": striped8(idx2),
    }


def reference(query, keys_words, keys_scales, gout, vals, share, fac, old, offs, offs2):
    idx = unstriped8(offs)
    idx2 = unstriped8(offs2)
    keysu = unpack_weight(keys_words, keys_scales, "e2m1")
    queryq = mxq(f64(query), 0, "e4m3")
    a = queryq.T @ keysu
    dl = (pick8(a, idx2, 16) - pick8(a, idx, 16)) * f64(share)
    df0 = np.zeros((Q, T))
    df0[np.arange(Q)[:, None], idx[np.arange(Q) % 128 // 16]] = dl
    s = a + df0
    p = np.exp(s - np.max(s, axis=1, keepdims=True))
    z = np.sum(p, axis=1, keepdims=True)
    goutq = mxq(f64(gout), 0, "e4m3")
    valsq = mxq(f64(vals), 0, "e4m3")
    c0 = goutq.T @ valsq
    dz = np.sum(c0 * p * f64(fac) / np.square(z) * (-1.0), axis=1, keepdims=True)
    dp = c0 / z * f64(fac) + dz
    ds = dp * p
    ddl = pick8(ds, idx, 16)
    e1 = ddl * f64(share)
    s1 = np.zeros((Q, T))
    s1[np.arange(Q)[:, None], idx2[np.arange(Q) % 128 // 16]] = e1
    e2 = ddl * f64(share) * (-1.0)
    s2 = np.zeros((Q, T))
    s2[np.arange(Q)[:, None], idx[np.arange(Q) % 128 // 16]] = e2
    da = ds + s1 + s2
    y = da * 1024.0 + f64(old)
    return y

@@ -1,0 +1,193 @@
+from contextlib import ExitStack
+
+import concourse.mybir as mybir
+
+F32 = mybir.dt.float32
+BF16 = mybir.dt.bfloat16
+I32 = mybir.dt.int32
+U32 = mybir.dt.uint32
+U16 = mybir.dt.uint16
+U8 = mybir.dt.uint8
+FP8X4 = mybir.dt.float8_e4m3fn_x4
+FP4X4 = mybir.dt.float4_e2m1fn_x4
+ALU = mybir.AluOpType
+ACT = mybir.ActivationFunctionType
+AXIS_X = mybir.AxisListType.X
+
+P = 128
+PACK = 4
+Q = 128
+T = 1024
+SLOTS = 512
+HALF = T // 2
+CHUNK = 256
+GAIN = 1024.0
+FLOPS = 2 * 2 * 512 * Q * T
+
+
+def interleave(copy, dst, src):
+    copy(
+        out=dst.rearrange("p (c i) j -> p c j i", i=4),
+        in_=src.rearrange("p j (c i) -> p c j i", i=4),
+    )
+
+
+def tile_attend_bborrowed_heads_kernel(tc, query, keys_words, keys_scales, gout, vals, share, fac, old, offs, offs2, out):
+    nc = tc.nc
+    with ExitStack() as ctx:
+        sb = ctx.enter_context(tc.tile_pool(name="sb", bufs=1))
+        ps = ctx.enter_context(tc.psum_pool(name="ps", bufs=1))
+
+        k_scale = sb.tile([P, T], U8, name="k_scale", align_bytes=64)
+        nc.vector.memset(k_scale[:].bitcast(I32), 0)
+        warm = sb.tile([P, 2], F32, name="warm")
+        nc.vector.memset(warm[:, 0:1], 0.0)
+
+        q_raw = sb.tile([P, PACK, Q], F32, name="q_raw")
+        nc.sync.dma_start(out=q_raw[:], in_=query.rearrange("(p j) q -> p j q", j=PACK))
+        for quad in range(4):
+            nc.sync.dma_start(
+                out=k_scale[32 * quad : 32 * quad + 4, :].bitcast(I32),
+                in_=keys_scales[0, 4 * quad : 4 * quad + 4, :].bitcast(I32),
+            )
+        k_words = sb.tile([P, 2 * T], U8, name="k_words", align_bytes=64)
+        nc.sync.dma_start(out=k_words[:].bitcast(I32), in_=keys_words[0].bitcast(I32))
+        share_col = sb.tile([P, 1], F32, name="share_col")
+        nc.scalar.dma_start(out=share_col[:], in_=share)
+        nc.scalar.activation(out=warm[:, 1:2], in_=warm[:, 0:1], func=ACT.Exp)
+        g_raw = sb.tile([P, PACK, Q], F32, name="g_raw")
+        vals_rows = vals.rearrange("(p j) t -> p j t", j=PACK)
+        v_raw = [sb.tile([P, PACK, CHUNK], F32, name="v_raw%d" % c) for c in range(T // CHUNK)]
+        list1 = sb.tile([P, SLOTS // 16], U16, name="list1")
+        list2 = sb.tile([P, SLOTS // 16], U16, name="list2")
+        nc.sync.dma_start(out=v_raw[0][:], in_=vals_rows[:, :, 0:CHUNK])
+        nc.sync.dma_start(list1[:], offs)
+        nc.sync.dma_start(out=v_raw[1][:], in_=vals_rows[:, :, CHUNK : 2 * CHUNK])
+        nc.sync.dma_start(list2[:], offs2)
+        nc.sync.dma_start(out=v_raw[2][:], in_=vals_rows[:, :, 2 * CHUNK : 3 * CHUNK])
+        nc.sync.dma_start(out=g_raw[:], in_=gout.rearrange("(p j) q -> p j q", j=PACK))
+        nc.sync.dma_start(out=v_raw[3][:], in_=vals_rows[:, :, 3 * CHUNK : 4 * CHUNK])
+        fac_rows = sb.tile([P, T], F32, name="fac_rows")
+        nc.sync.dma_start(out=fac_rows[:], in_=fac[0].partition_broadcast(P))
+        old_sb = sb.tile([P, T], F32, name="old_sb")
+        nc.sync.dma_start(out=old_sb[:], in_=old)
+
+        placed1 = sb.tile([P, T], F32, name="placed1")
+        placed2 = sb.tile([P, T], F32, name="placed2")
+        nc.vector.memset(placed1[:], 0.0)
+        nc.vector.memset(placed2[:], 0.0)
+
+        q_bf = sb.tile([P, Q, PACK], BF16, name="q_bf", align_bytes=64)
+        interleave(nc.vector.tensor_copy, q_bf[:], q_raw[:])
+        q_code = sb.tile([P, Q], U32, name="q_code", align_bytes=64)
+        q_scale = sb.tile([P, Q], U8, name="q_scale", align_bytes=64)
+        nc.vector.quantize_mx(out=q_code[:].bitcast(FP8X4), scales=q_scale[:], in_=q_bf[:].rearrange("p q j -> p (q j)"))
+
+        a_sb = sb.tile([P, T], F32, name="a_sb", tag="a_then_cf")
+        for b in range(T // CHUNK):
+            a_ps = ps.tile([P, CHUNK], F32, name="a_ps%d" % b)
+            cols = slice(b * CHUNK, (b + 1) * CHUNK)
+            nc.tensor.matmul_mx(
+                out=a_ps[:],
+                lhsT=q_code[:].bitcast(FP8X4),
+                lhsT_scale=q_scale[:],
+                rhs=k_words[:, 2 * b * CHUNK : 2 * (b + 1) * CHUNK].bitcast(FP4X4),
+                rhs_scale=k_scale[:, cols],
+                start=True,
+                stop=True,
+            )
+            nc.vector.tensor_copy(out=a_sb[:, cols], in_=a_ps[:])
+
+        share_row = sb.tile([P, SLOTS], F32, name="share_row")
+        nc.scalar.copy(out=share_row[:], in_=share_col[:].to_broadcast([P, SLOTS]))
+
+        gain_row = sb.tile([P, SLOTS], F32, name="gain_row")
+        nc.scalar.activation(out=gain_row[:], in_=share_row[:], func=ACT.Copy, scale=GAIN)
+        v_code = sb.tile([P, T], U32, name="v_code", align_bytes=64)
+        v_scale = sb.tile([P, T], U8, name="v_scale", align_bytes=64)
+        v_bf0 = sb.tile([P, CHUNK, PACK], BF16, name="v_bf0", tag="v_then_diff", align_bytes=64)
+        v_bf1 = sb.tile([P, CHUNK, PACK], BF16, name="v_bf1", align_bytes=64)
+        v_bf23 = sb.tile([P, 2, CHUNK, PACK], BF16, name="v_bf23", tag="v_then_s", align_bytes=64)
+        v_bf = [v_bf0[:], v_bf1[:], v_bf23[:, 0], v_bf23[:, 1]]
+
+        def quantise_values(c):
+            cols = slice(c * CHUNK, (c + 1) * CHUNK)
+            interleave(nc.scalar.copy, v_bf[c], v_raw[c][:])
+            nc.vector.quantize_mx(
+                out=v_code[:, cols].bitcast(FP8X4), scales=v_scale[:, cols], in_=v_bf[c].rearrange("p t j -> p (t j)")
+            )
+
+        own = sb.tile([P, SLOTS], F32, name="own")
+        nc.vector.tensor_copy(own[:], a_sb[:].indirect(list1[:]))
+        quantise_values(0)
+        diff = sb.tile([P, SLOTS], F32, name="diff", tag="v_then_diff", align_bytes=64)
+        nc.vector.tensor_tensor(diff[:], a_sb[:].indirect(list2[:]), own[:], ALU.subtract)
+        nc.vector.tensor_tensor(placed1[:].indirect(list1[:]), diff[:], share_row[:], ALU.mult)
+        quantise_values(1)
+        quantise_values(2)
+        g_bf = sb.tile([P, Q, PACK], BF16, name="g_bf", align_bytes=64)
+        interleave(nc.scalar.copy, g_bf[:], g_raw[:])
+        g_code = sb.tile([P, Q], U32, name="g_code", align_bytes=64)
+        g_scale = sb.tile([P, Q], U8, name="g_scale", align_bytes=64)
+        nc.vector.quantize_mx(out=g_code[:].bitcast(FP8X4), scales=g_scale[:], in_=g_bf[:].rearrange("p q j -> p (q j)"))
+
+        quantise_values(3)
+        c_ps = [ps.tile([P, HALF], F32, name="c_ps%d" % h) for h in range(2)]
+        for h in range(2):
+            cols = slice(h * HALF, (h + 1) * HALF)
+            nc.tensor.matmul_mx(
+                out=c_ps[h][:],
+                lhsT=g_code[:].bitcast(FP8X4),
+                lhsT_scale=g_scale[:],
+                rhs=v_code[:, cols].bitcast(FP8X4),
+                rhs_scale=v_scale[:, cols],
+                start=True,
+                stop=True,
+            )
+
+        s = sb.tile([P, T], F32, name="s", tag="v_then_s", align_bytes=64)
+        nc.vector.tensor_tensor(s[:], a_sb[:], placed1[:], ALU.add)
+        neg_max = sb.tile([P, 1], F32, name="neg_max")
+        nc.vector.tensor_reduce(out=neg_max[:], in_=s[:], axis=AXIS_X, op=ALU.max, negate=True)
+        p = sb.tile([P, T], F32, name="p")
+        cf = sb.tile([P, T], F32, name="cf", tag="a_then_cf")
+        z_half = sb.tile([P, 2], F32, name="z_half")
+        w_half = sb.tile([P, 2], F32, name="w_half")
+        for h in range(2):
+            cols = slice(h * HALF, (h + 1) * HALF)
+            nc.scalar.activation(out=p[:, cols], in_=s[:, cols], func=ACT.Exp, bias=neg_max[:], accum_out=z_half[:, h : h + 1])
+        for h in range(2):
+            cols = slice(h * HALF, (h + 1) * HALF)
+            nc.vector.tensor_tensor(cf[:, cols], c_ps[h][:], fac_rows[:, cols], ALU.mult)
+        weighted = sb.tile([P, T], F32, name="weighted")
+        z = sb.tile([P, 1], F32, name="z")
+        inv_z = sb.tile([P, 1], F32, name="inv_z")
+        nc.vector.scalar_tensor_tensor(weighted[:, 0:HALF], cf[:, 0:HALF], 1.0, p[:, 0:HALF], ALU.mult, ALU.mult, accum_out=w_half[:, 0:1])
+        nc.vector.tensor_tensor(z[:], z_half[:, 0:1], z_half[:, 1:2], ALU.add)
+        nc.vector.reciprocal(inv_z[:], z[:])
+        nc.vector.scalar_tensor_tensor(weighted[:, HALF:T], cf[:, HALF:T], 1.0, p[:, HALF:T], ALU.mult, ALU.mult, accum_out=w_half[:, 1:2])
+        mean = sb.tile([P, 1], F32, name="mean")
+        nc.vector.tensor_scalar(mean[:], w_half[:, 0:1], w_half[:, 1:2], inv_z[:], ALU.add, ALU.mult)
+        prob = sb.tile([P, T], F32, name="prob")
+        ds = sb.tile([P, T], F32, name="ds")
+        for h in range(2):
+            cols = slice(h * HALF, (h + 1) * HALF)
+            nc.scalar.activation(out=prob[:, cols], in_=p[:, cols], func=ACT.Copy, scale=inv_z[:])
+            nc.vector.scalar_tensor_tensor(ds[:, cols], cf[:, cols], mean[:], prob[:, cols], ALU.subtract, ALU.mult)
+
+        e1 = sb.tile([P, SLOTS], F32, name="e1")
+        nc.vector.tensor_tensor(e1[:], ds[:].indirect(list1[:]), gain_row[:], ALU.mult)
+        base = sb.tile([P, T], F32, name="base")
+        nc.vector.scalar_tensor_tensor(base[:], ds[:], GAIN, old_sb[:], ALU.mult, ALU.add)
+        e2 = sb.tile([P, SLOTS], F32, name="e2")
+        nc.scalar.activation(out=e2[:], in_=e1[:], func=ACT.Copy, scale=-1.0)
+        nc.vector.tensor_copy(placed2[:].indirect(list2[:]), e1[:])
+        nc.vector.tensor_copy(placed1[:].indirect(list1[:]), e2[:])
+        part = sb.tile([P, T], F32, name="part")
+        nc.vector.tensor_tensor(part[:], base[:], placed2[:], ALU.add)
+        y = sb.tile([P, T], F32, name="y")
+        for c in range(T // CHUNK):
+            cols = slice(c * CHUNK, (c + 1) * CHUNK)
+            nc.vector.tensor_tensor(y[:, cols], part[:, cols], placed1[:, cols], ALU.add)
+            queue = nc.sync if c % 2 == 0 else nc.scalar
+            queue.dma_start(out=out[:, cols], in_=y[:, cols])

@@ -1,6 +1,7 @@
 from contextlib import ExitStack
 
 import concourse.mybir as mybir
+from concourse.masks import make_identity
 
 F32 = mybir.dt.float32
 BF16 = mybir.dt.bfloat16
@@ -19,17 +20,33 @@ PACK = 4
 Q = 128
 T = 1024
 SLOTS = 512
+GROUP = 16
+QUADRANT = 32
 HALF = T // 2
 CHUNK = 256
+CHUNKS = T // CHUNK
+BLOCKS = T // P
+BANK_BLOCKS = HALF // P
+CHUNK_BLOCKS = CHUNK // P
+LINE = 4
+LATE = 16
 GAIN = 1024.0
-FLOPS = 2 * 2 * 512 * Q * T
+FLOPS = 2 * 2 * P * PACK * Q * T
+
+SCORE_BANK = 0
+PRODUCT_BANK = 4
+WEIGHED_BANK = 6
 
 
 def interleave(copy, dst, src):
     copy(
-        out=dst.rearrange("p (c i) j -> p c j i", i=4),
-        in_=src.rearrange("p j (c i) -> p c j i", i=4),
+        out=dst.rearrange("p (c i) j -> p c j i", i=LINE),
+        in_=src.rearrange("p j (c i) -> p c j i", i=LINE),
     )
+
+
+def span(i, width):
+    return slice(i * width, (i + 1) * width)
 
 
 def tile_attend_bborrowed_heads_kernel(tc, query, keys_words, keys_scales, gout, vals, share, fac, old, offs, offs2, out):
@@ -38,156 +55,212 @@ def tile_attend_bborrowed_heads_kernel(tc, query, keys_words, keys_scales, gout,
         sb = ctx.enter_context(tc.tile_pool(name="sb", bufs=1))
         ps = ctx.enter_context(tc.psum_pool(name="ps", bufs=1))
 
+        def bank(name, number, width):
+            return ps.tile([P, width], F32, name=name, tag="bank%d" % number)
+
+        def quantise(codes, scales, grouped):
+            nc.vector.quantize_mx(out=codes.bitcast(FP8X4), scales=scales, in_=grouped.rearrange("p c j -> p (c j)"))
+
         k_scale = sb.tile([P, T], U8, name="k_scale", align_bytes=64)
         nc.vector.memset(k_scale[:].bitcast(I32), 0)
-        warm = sb.tile([P, 2], F32, name="warm")
-        nc.vector.memset(warm[:, 0:1], 0.0)
 
         q_raw = sb.tile([P, PACK, Q], F32, name="q_raw")
         nc.sync.dma_start(out=q_raw[:], in_=query.rearrange("(p j) q -> p j q", j=PACK))
-        for quad in range(4):
+        for quad in range(P // QUADRANT):
             nc.sync.dma_start(
-                out=k_scale[32 * quad : 32 * quad + 4, :].bitcast(I32),
-                in_=keys_scales[0, 4 * quad : 4 * quad + 4, :].bitcast(I32),
+                out=k_scale[QUADRANT * quad : QUADRANT * quad + PACK, :].bitcast(I32),
+                in_=keys_scales[0, span(quad, PACK), :].bitcast(I32),
             )
         k_words = sb.tile([P, 2 * T], U8, name="k_words", align_bytes=64)
         nc.sync.dma_start(out=k_words[:].bitcast(I32), in_=keys_words[0].bitcast(I32))
         share_col = sb.tile([P, 1], F32, name="share_col")
         nc.scalar.dma_start(out=share_col[:], in_=share)
-        nc.scalar.activation(out=warm[:, 1:2], in_=warm[:, 0:1], func=ACT.Exp)
-        g_raw = sb.tile([P, PACK, Q], F32, name="g_raw")
+        shared = sb.tile([P, 2 * SLOTS - LATE], F32, name="shared")
+        share_row = shared[:, 0:SLOTS]
+        g_raw = shared[:, SLOTS - LATE :].rearrange("p (j q) -> p j q", j=PACK)
         vals_rows = vals.rearrange("(p j) t -> p j t", j=PACK)
-        v_raw = [sb.tile([P, PACK, CHUNK], F32, name="v_raw%d" % c) for c in range(T // CHUNK)]
-        list1 = sb.tile([P, SLOTS // 16], U16, name="list1")
-        list2 = sb.tile([P, SLOTS // 16], U16, name="list2")
-        nc.sync.dma_start(out=v_raw[0][:], in_=vals_rows[:, :, 0:CHUNK])
+        v_raw = [sb.tile([P, PACK, CHUNK], F32, name="v_raw%d" % c, tag="v_raw%d" % c) for c in range(CHUNKS)]
+        list1 = sb.tile([P, SLOTS // GROUP], U16, name="list1")
+        list2 = sb.tile([P, SLOTS // GROUP], U16, name="list2")
+        fac_rows = sb.tile([P, P], F32, name="fac_rows")
+        nc.gpsimd.memset(fac_rows[:], 0.0)
+
+        def load_values(c):
+            nc.sync.dma_start(out=v_raw[c][:], in_=vals_rows[:, :, span(c, CHUNK)])
+
+        load_values(0)
         nc.sync.dma_start(list1[:], offs)
-        nc.sync.dma_start(out=v_raw[1][:], in_=vals_rows[:, :, CHUNK : 2 * CHUNK])
+        load_values(1)
         nc.sync.dma_start(list2[:], offs2)
-        nc.sync.dma_start(out=v_raw[2][:], in_=vals_rows[:, :, 2 * CHUNK : 3 * CHUNK])
-        nc.sync.dma_start(out=g_raw[:], in_=gout.rearrange("(p j) q -> p j q", j=PACK))
-        nc.sync.dma_start(out=v_raw[3][:], in_=vals_rows[:, :, 3 * CHUNK : 4 * CHUNK])
-        fac_rows = sb.tile([P, T], F32, name="fac_rows")
-        nc.sync.dma_start(out=fac_rows[:], in_=fac[0].partition_broadcast(P))
+        nc.sync.dma_start(out=fac_rows[0:BLOCKS, :], in_=fac.rearrange("o (b t) -> (o b) t", t=P))
+        nc.sync.dma_start(out=g_raw, in_=gout.rearrange("(p j) q -> p j q", j=PACK))
+        load_values(2)
+        load_values(3)
         old_sb = sb.tile([P, T], F32, name="old_sb")
         nc.sync.dma_start(out=old_sb[:], in_=old)
+
+        identity = sb.tile([P, P], F32, name="identity")
+        make_identity(nc, identity[:])
+
+        def turn(dst, src, start, stop):
+            nc.tensor.matmul(dst, lhsT=src, rhs=identity[:], is_transpose=True, start=start, stop=stop)
+
+        def turn_half(dst, src, opens, closes):
+            for b in range(BANK_BLOCKS):
+                turn(dst[:, span(b, P)], src[:, span(b, P)], opens and b == 0, closes and b == BANK_BLOCKS - 1)
 
         placed1 = sb.tile([P, T], F32, name="placed1")
         placed2 = sb.tile([P, T], F32, name="placed2")
         nc.vector.memset(placed1[:], 0.0)
         nc.vector.memset(placed2[:], 0.0)
 
+        nc.scalar.copy(out=share_row[:, 0 : SLOTS - LATE], in_=share_col[:].to_broadcast([P, SLOTS - LATE]))
+        neg_share_row = sb.tile([P, SLOTS], F32, name="neg_share_row")
+        nc.scalar.activation(out=neg_share_row[:], in_=share_col[:].to_broadcast([P, SLOTS]), func=ACT.Copy, scale=-1.0)
+
         q_bf = sb.tile([P, Q, PACK], BF16, name="q_bf", align_bytes=64)
         interleave(nc.vector.tensor_copy, q_bf[:], q_raw[:])
         q_code = sb.tile([P, Q], U32, name="q_code", align_bytes=64)
         q_scale = sb.tile([P, Q], U8, name="q_scale", align_bytes=64)
-        nc.vector.quantize_mx(out=q_code[:].bitcast(FP8X4), scales=q_scale[:], in_=q_bf[:].rearrange("p q j -> p (q j)"))
+        quantise(q_code[:], q_scale[:], q_bf[:])
 
-        a_sb = sb.tile([P, T], F32, name="a_sb", tag="a_then_cf")
-        for b in range(T // CHUNK):
-            a_ps = ps.tile([P, CHUNK], F32, name="a_ps%d" % b)
-            cols = slice(b * CHUNK, (b + 1) * CHUNK)
+        a_sb = sb.tile([P, T], F32, name="a_sb")
+        for c in range(CHUNKS):
+            a_ps = bank("a_ps%d" % c, SCORE_BANK + c, CHUNK)
             nc.tensor.matmul_mx(
                 out=a_ps[:],
                 lhsT=q_code[:].bitcast(FP8X4),
                 lhsT_scale=q_scale[:],
-                rhs=k_words[:, 2 * b * CHUNK : 2 * (b + 1) * CHUNK].bitcast(FP4X4),
-                rhs_scale=k_scale[:, cols],
+                rhs=k_words[:, span(c, 2 * CHUNK)].bitcast(FP4X4),
+                rhs_scale=k_scale[:, span(c, CHUNK)],
                 start=True,
                 stop=True,
             )
-            nc.vector.tensor_copy(out=a_sb[:, cols], in_=a_ps[:])
+            nc.vector.tensor_copy(out=a_sb[:, span(c, CHUNK)], in_=a_ps[:])
 
-        share_row = sb.tile([P, SLOTS], F32, name="share_row")
-        nc.scalar.copy(out=share_row[:], in_=share_col[:].to_broadcast([P, SLOTS]))
-
-        gain_row = sb.tile([P, SLOTS], F32, name="gain_row")
-        nc.scalar.activation(out=gain_row[:], in_=share_row[:], func=ACT.Copy, scale=GAIN)
         v_code = sb.tile([P, T], U32, name="v_code", align_bytes=64)
         v_scale = sb.tile([P, T], U8, name="v_scale", align_bytes=64)
-        v_bf0 = sb.tile([P, CHUNK, PACK], BF16, name="v_bf0", tag="v_then_diff", align_bytes=64)
-        v_bf1 = sb.tile([P, CHUNK, PACK], BF16, name="v_bf1", align_bytes=64)
-        v_bf23 = sb.tile([P, 2, CHUNK, PACK], BF16, name="v_bf23", tag="v_then_s", align_bytes=64)
-        v_bf = [v_bf0[:], v_bf1[:], v_bf23[:, 0], v_bf23[:, 1]]
+        v_bf = [sb.tile([P, CHUNK, PACK], BF16, name="v_bf%d" % c, align_bytes=64) for c in range(CHUNKS)]
+
+        def interleave_values(c):
+            interleave(nc.scalar.copy, v_bf[c][:], v_raw[c][:])
 
         def quantise_values(c):
-            cols = slice(c * CHUNK, (c + 1) * CHUNK)
-            interleave(nc.scalar.copy, v_bf[c], v_raw[c][:])
-            nc.vector.quantize_mx(
-                out=v_code[:, cols].bitcast(FP8X4), scales=v_scale[:, cols], in_=v_bf[c].rearrange("p t j -> p (t j)")
-            )
+            quantise(v_code[:, span(c, CHUNK)], v_scale[:, span(c, CHUNK)], v_bf[c][:])
+
+        fac_ps = bank("fac_ps", WEIGHED_BANK, P)
+        turn(fac_ps[:], fac_rows[:], True, True)
+        fac_cols = sb.tile([P, BLOCKS], F32, name="fac_cols")
 
         own = sb.tile([P, SLOTS], F32, name="own")
         nc.vector.tensor_copy(own[:], a_sb[:].indirect(list1[:]))
-        quantise_values(0)
-        diff = sb.tile([P, SLOTS], F32, name="diff", tag="v_then_diff", align_bytes=64)
+        diff = sb.tile([P, SLOTS], F32, name="diff")
         nc.vector.tensor_tensor(diff[:], a_sb[:].indirect(list2[:]), own[:], ALU.subtract)
-        nc.vector.tensor_tensor(placed1[:].indirect(list1[:]), diff[:], share_row[:], ALU.mult)
-        quantise_values(1)
-        quantise_values(2)
+        for c in range(CHUNKS // 2):
+            interleave_values(c)
+            quantise_values(c)
         g_bf = sb.tile([P, Q, PACK], BF16, name="g_bf", align_bytes=64)
-        interleave(nc.scalar.copy, g_bf[:], g_raw[:])
+        interleave(nc.scalar.copy, g_bf[:], g_raw)
         g_code = sb.tile([P, Q], U32, name="g_code", align_bytes=64)
         g_scale = sb.tile([P, Q], U8, name="g_scale", align_bytes=64)
-        nc.vector.quantize_mx(out=g_code[:].bitcast(FP8X4), scales=g_scale[:], in_=g_bf[:].rearrange("p q j -> p (q j)"))
+        quantise(g_code[:], g_scale[:], g_bf[:])
+        nc.scalar.copy(out=share_row[:, SLOTS - LATE :], in_=share_col[:].to_broadcast([P, LATE]))
+        nc.scalar.copy(out=fac_cols[:], in_=fac_ps[:, 0:BLOCKS])
+        nc.vector.tensor_tensor(placed1[:].indirect(list1[:]), diff[:], share_row, ALU.mult)
 
-        quantise_values(3)
-        c_ps = [ps.tile([P, HALF], F32, name="c_ps%d" % h) for h in range(2)]
-        for h in range(2):
-            cols = slice(h * HALF, (h + 1) * HALF)
-            nc.tensor.matmul_mx(
-                out=c_ps[h][:],
-                lhsT=g_code[:].bitcast(FP8X4),
-                lhsT_scale=g_scale[:],
-                rhs=v_code[:, cols].bitcast(FP8X4),
-                rhs_scale=v_scale[:, cols],
-                start=True,
-                stop=True,
-            )
+        cf_turned = sb.tile([P, T], F32, name="cf_turned")
+        cf = [bank("cf%d" % h, WEIGHED_BANK + h, HALF) for h in range(2)]
 
-        s = sb.tile([P, T], F32, name="s", tag="v_then_s", align_bytes=64)
+        def weigh(c):
+            c_ps = bank("c_ps%d" % c, PRODUCT_BANK + c % 2, CHUNK)
+            blocks = range(CHUNK_BLOCKS * c, CHUNK_BLOCKS * (c + 1))
+            for block in blocks:
+                nc.tensor.matmul_mx(
+                    out=c_ps[:, span(block % CHUNK_BLOCKS, P)],
+                    lhsT=v_code[:, span(block, P)].bitcast(FP8X4),
+                    lhsT_scale=v_scale[:, span(block, P)],
+                    rhs=g_code[:].bitcast(FP8X4),
+                    rhs_scale=g_scale[:],
+                    start=True,
+                    stop=True,
+                )
+            for block in blocks:
+                nc.scalar.activation(
+                    out=cf_turned[:, span(block, P)],
+                    in_=c_ps[:, span(block % CHUNK_BLOCKS, P)],
+                    func=ACT.Copy,
+                    scale=fac_cols[:, block : block + 1],
+                )
+            for block in blocks:
+                turn(cf[block // BANK_BLOCKS][:, span(block % BANK_BLOCKS, P)], cf_turned[:, span(block, P)], True, True)
+
+        last = CHUNKS - 1
+        interleave_values(last - 1)
+        quantise_values(last - 1)
+        interleave_values(last)
+        s = sb.tile([P, T], F32, name="s", tag="v_raw%d" % last)
         nc.vector.tensor_tensor(s[:], a_sb[:], placed1[:], ALU.add)
+        quantise_values(last)
         neg_max = sb.tile([P, 1], F32, name="neg_max")
         nc.vector.tensor_reduce(out=neg_max[:], in_=s[:], axis=AXIS_X, op=ALU.max, negate=True)
+        for c in range(CHUNKS):
+            weigh(c)
+
         p = sb.tile([P, T], F32, name="p")
-        cf = sb.tile([P, T], F32, name="cf", tag="a_then_cf")
         z_half = sb.tile([P, 2], F32, name="z_half")
         w_half = sb.tile([P, 2], F32, name="w_half")
         for h in range(2):
-            cols = slice(h * HALF, (h + 1) * HALF)
-            nc.scalar.activation(out=p[:, cols], in_=s[:, cols], func=ACT.Exp, bias=neg_max[:], accum_out=z_half[:, h : h + 1])
-        for h in range(2):
-            cols = slice(h * HALF, (h + 1) * HALF)
-            nc.vector.tensor_tensor(cf[:, cols], c_ps[h][:], fac_rows[:, cols], ALU.mult)
+            nc.scalar.activation(
+                out=p[:, span(h, HALF)], in_=s[:, span(h, HALF)], func=ACT.Exp, bias=neg_max[:], accum_out=z_half[:, h : h + 1]
+            )
         weighted = sb.tile([P, T], F32, name="weighted")
         z = sb.tile([P, 1], F32, name="z")
         inv_z = sb.tile([P, 1], F32, name="inv_z")
-        nc.vector.scalar_tensor_tensor(weighted[:, 0:HALF], cf[:, 0:HALF], 1.0, p[:, 0:HALF], ALU.mult, ALU.mult, accum_out=w_half[:, 0:1])
+
+        def weighted_sum(h):
+            cols = span(h, HALF)
+            nc.vector.scalar_tensor_tensor(
+                weighted[:, cols], cf[h][:], 1.0, p[:, cols], ALU.mult, ALU.mult, accum_out=w_half[:, h : h + 1]
+            )
+
+        weighted_sum(0)
         nc.vector.tensor_tensor(z[:], z_half[:, 0:1], z_half[:, 1:2], ALU.add)
         nc.vector.reciprocal(inv_z[:], z[:])
-        nc.vector.scalar_tensor_tensor(weighted[:, HALF:T], cf[:, HALF:T], 1.0, p[:, HALF:T], ALU.mult, ALU.mult, accum_out=w_half[:, 1:2])
+        weighted_sum(1)
         mean = sb.tile([P, 1], F32, name="mean")
         nc.vector.tensor_scalar(mean[:], w_half[:, 0:1], w_half[:, 1:2], inv_z[:], ALU.add, ALU.mult)
         prob = sb.tile([P, T], F32, name="prob")
         ds = sb.tile([P, T], F32, name="ds")
         for h in range(2):
-            cols = slice(h * HALF, (h + 1) * HALF)
-            nc.scalar.activation(out=prob[:, cols], in_=p[:, cols], func=ACT.Copy, scale=inv_z[:])
-            nc.vector.scalar_tensor_tensor(ds[:, cols], cf[:, cols], mean[:], prob[:, cols], ALU.subtract, ALU.mult)
+            nc.scalar.activation(out=prob[:, span(h, HALF)], in_=p[:, span(h, HALF)], func=ACT.Copy, scale=inv_z[:])
+            nc.vector.scalar_tensor_tensor(ds[:, span(h, HALF)], cf[h][:], mean[:], prob[:, span(h, HALF)], ALU.subtract, ALU.mult)
 
-        e1 = sb.tile([P, SLOTS], F32, name="e1")
-        nc.vector.tensor_tensor(e1[:], ds[:].indirect(list1[:]), gain_row[:], ALU.mult)
-        base = sb.tile([P, T], F32, name="base")
-        nc.vector.scalar_tensor_tensor(base[:], ds[:], GAIN, old_sb[:], ALU.mult, ALU.add)
-        e2 = sb.tile([P, SLOTS], F32, name="e2")
-        nc.scalar.activation(out=e2[:], in_=e1[:], func=ACT.Copy, scale=-1.0)
-        nc.vector.tensor_copy(placed2[:].indirect(list2[:]), e1[:])
-        nc.vector.tensor_copy(placed1[:].indirect(list1[:]), e2[:])
-        part = sb.tile([P, T], F32, name="part")
-        nc.vector.tensor_tensor(part[:], base[:], placed2[:], ALU.add)
+        ddl = sb.tile([P, SLOTS], F32, name="ddl")
+        nc.vector.tensor_copy(ddl[:], ds[:].indirect(list1[:]))
+        nc.vector.tensor_tensor(placed2[:].indirect(list2[:]), ddl[:], share_row, ALU.mult)
+        nc.vector.tensor_tensor(placed1[:].indirect(list1[:]), ddl[:], neg_share_row[:], ALU.mult)
+
+        old_turned = sb.tile([P, T], F32, name="old_turned")
+        for h in range(2):
+            stage = bank("old_stage%d" % h, WEIGHED_BANK + h, HALF)
+            turn_half(stage, old_sb[:, span(h, HALF)], True, True)
+            nc.scalar.copy(out=old_turned[:, span(h, HALF)], in_=stage[:])
+        part = [bank("part%d" % h, SCORE_BANK + 2 + h, HALF) for h in range(2)]
+        inner = [bank("inner%d" % h, SCORE_BANK + h, HALF) for h in range(2)]
+        for h in range(2):
+            turn_half(part[h], old_turned[:, span(h, HALF)], True, False)
+        for h in range(2):
+            turn_half(inner[h], ds[:, span(h, HALF)], True, False)
+        inner_turned = sb.tile([P, T], F32, name="inner_turned")
+        for h in range(2):
+            turn_half(inner[h], placed2[:, span(h, HALF)], False, True)
+            nc.scalar.activation(out=inner_turned[:, span(h, HALF)], in_=inner[h][:], func=ACT.Copy, scale=GAIN)
+        for h in range(2):
+            turn_half(part[h], inner_turned[:, span(h, HALF)], False, True)
+
         y = sb.tile([P, T], F32, name="y")
-        for c in range(T // CHUNK):
-            cols = slice(c * CHUNK, (c + 1) * CHUNK)
-            nc.vector.tensor_tensor(y[:, cols], part[:, cols], placed1[:, cols], ALU.add)
+        for c in range(CHUNKS):
+            cols = span(c, CHUNK)
+            nc.vector.scalar_tensor_tensor(y[:, cols], placed1[:, cols], GAIN, part[c // 2][:, span(c % 2, CHUNK)], ALU.mult, ALU.add)
             queue = nc.sync if c % 2 == 0 else nc.scalar
             queue.dma_start(out=out[:, cols], in_=y[:, cols])

from contextlib import ExitStack

import concourse.mybir as mybir
from concourse.masks import make_identity

F32 = mybir.dt.float32
BF16 = mybir.dt.bfloat16
I32 = mybir.dt.int32
U32 = mybir.dt.uint32
U16 = mybir.dt.uint16
U8 = mybir.dt.uint8
FP8X4 = mybir.dt.float8_e4m3fn_x4
FP4X4 = mybir.dt.float4_e2m1fn_x4
ALU = mybir.AluOpType
ACT = mybir.ActivationFunctionType
AXIS_X = mybir.AxisListType.X

P = 128
PACK = 4
Q = 128
T = 1024
SLOTS = 512
GROUP = 16
QUADRANT = 32
HALF = T // 2
CHUNK = 256
CHUNKS = T // CHUNK
BLOCKS = T // P
BANK_BLOCKS = HALF // P
CHUNK_BLOCKS = CHUNK // P
LINE = 4
LATE = 16
GAIN = 1024.0
FLOPS = 2 * 2 * P * PACK * Q * T

SCORE_BANK = 0
PRODUCT_BANK = 4
WEIGHED_BANK = 6


def interleave(copy, dst, src):
    copy(
        out=dst.rearrange("p (c i) j -> p c j i", i=LINE),
        in_=src.rearrange("p j (c i) -> p c j i", i=LINE),
    )


def span(i, width):
    return slice(i * width, (i + 1) * width)


def tile_attend_bborrowed_heads_kernel(tc, query, keys_words, keys_scales, gout, vals, share, fac, old, offs, offs2, out):
    nc = tc.nc
    with ExitStack() as ctx:
        sb = ctx.enter_context(tc.tile_pool(name="sb", bufs=1))
        ps = ctx.enter_context(tc.psum_pool(name="ps", bufs=1))

        def bank(name, number, width):
            return ps.tile([P, width], F32, name=name, tag="bank%d" % number)

        def quantise(codes, scales, grouped):
            nc.vector.quantize_mx(out=codes.bitcast(FP8X4), scales=scales, in_=grouped.rearrange("p c j -> p (c j)"))

        k_scale = sb.tile([P, T], U8, name="k_scale", align_bytes=64)
        nc.vector.memset(k_scale[:].bitcast(I32), 0)

        q_raw = sb.tile([P, PACK, Q], F32, name="q_raw")
        nc.sync.dma_start(out=q_raw[:], in_=query.rearrange("(p j) q -> p j q", j=PACK))
        for quad in range(P // QUADRANT):
            nc.sync.dma_start(
                out=k_scale[QUADRANT * quad : QUADRANT * quad + PACK, :].bitcast(I32),
                in_=keys_scales[0, span(quad, PACK), :].bitcast(I32),
            )
        k_words = sb.tile([P, 2 * T], U8, name="k_words", align_bytes=64)
        nc.sync.dma_start(out=k_words[:].bitcast(I32), in_=keys_words[0].bitcast(I32))
        share_col = sb.tile([P, 1], F32, name="share_col")
        nc.scalar.dma_start(out=share_col[:], in_=share)
        shared = sb.tile([P, 2 * SLOTS - LATE], F32, name="shared")
        share_row = shared[:, 0:SLOTS]
        g_raw = shared[:, SLOTS - LATE :].rearrange("p (j q) -> p j q", j=PACK)
        vals_rows = vals.rearrange("(p j) t -> p j t", j=PACK)
        v_raw = [sb.tile([P, PACK, CHUNK], F32, name="v_raw%d" % c, tag="v_raw%d" % c) for c in range(CHUNKS)]
        list1 = sb.tile([P, SLOTS // GROUP], U16, name="list1")
        list2 = sb.tile([P, SLOTS // GROUP], U16, name="list2")
        fac_rows = sb.tile([P, P], F32, name="fac_rows")
        nc.gpsimd.memset(fac_rows[:], 0.0)

        def load_values(c):
            nc.sync.dma_start(out=v_raw[c][:], in_=vals_rows[:, :, span(c, CHUNK)])

        load_values(0)
        nc.sync.dma_start(list1[:], offs)
        load_values(1)
        nc.sync.dma_start(list2[:], offs2)
        nc.sync.dma_start(out=fac_rows[0:BLOCKS, :], in_=fac.rearrange("o (b t) -> (o b) t", t=P))
        nc.sync.dma_start(out=g_raw, in_=gout.rearrange("(p j) q -> p j q", j=PACK))
        load_values(2)
        load_values(3)
        old_sb = sb.tile([P, T], F32, name="old_sb")
        nc.sync.dma_start(out=old_sb[:], in_=old)

        identity = sb.tile([P, P], F32, name="identity")
        make_identity(nc, identity[:])

        def turn(dst, src, start, stop):
            nc.tensor.matmul(dst, lhsT=src, rhs=identity[:], is_transpose=True, start=start, stop=stop)

        def turn_half(dst, src, opens, closes):
            for b in range(BANK_BLOCKS):
                turn(dst[:, span(b, P)], src[:, span(b, P)], opens and b == 0, closes and b == BANK_BLOCKS - 1)

        placed1 = sb.tile([P, T], F32, name="placed1")
        placed2 = sb.tile([P, T], F32, name="placed2")
        nc.vector.memset(placed1[:], 0.0)
        nc.vector.memset(placed2[:], 0.0)

        nc.scalar.copy(out=share_row[:, 0 : SLOTS - LATE], in_=share_col[:].to_broadcast([P, SLOTS - LATE]))
        neg_share_row = sb.tile([P, SLOTS], F32, name="neg_share_row")
        nc.scalar.activation(out=neg_share_row[:], in_=share_col[:].to_broadcast([P, SLOTS]), func=ACT.Copy, scale=-1.0)

        q_bf = sb.tile([P, Q, PACK], BF16, name="q_bf", align_bytes=64)
        interleave(nc.vector.tensor_copy, q_bf[:], q_raw[:])
        q_code = sb.tile([P, Q], U32, name="q_code", align_bytes=64)
        q_scale = sb.tile([P, Q], U8, name="q_scale", align_bytes=64)
        quantise(q_code[:], q_scale[:], q_bf[:])

        a_sb = sb.tile([P, T], F32, name="a_sb")
        for c in range(CHUNKS):
            a_ps = bank("a_ps%d" % c, SCORE_BANK + c, CHUNK)
            nc.tensor.matmul_mx(
                out=a_ps[:],
                lhsT=q_code[:].bitcast(FP8X4),
                lhsT_scale=q_scale[:],
                rhs=k_words[:, span(c, 2 * CHUNK)].bitcast(FP4X4),
                rhs_scale=k_scale[:, span(c, CHUNK)],
                start=True,
                stop=True,
            )
            nc.vector.tensor_copy(out=a_sb[:, span(c, CHUNK)], in_=a_ps[:])

        v_code = sb.tile([P, T], U32, name="v_code", align_bytes=64)
        v_scale = sb.tile([P, T], U8, name="v_scale", align_bytes=64)
        v_bf = [sb.tile([P, CHUNK, PACK], BF16, name="v_bf%d" % c, align_bytes=64) for c in range(CHUNKS)]

        def interleave_values(c):
            interleave(nc.scalar.copy, v_bf[c][:], v_raw[c][:])

        def quantise_values(c):
            quantise(v_code[:, span(c, CHUNK)], v_scale[:, span(c, CHUNK)], v_bf[c][:])

        fac_ps = bank("fac_ps", WEIGHED_BANK, P)
        turn(fac_ps[:], fac_rows[:], True, True)
        fac_cols = sb.tile([P, BLOCKS], F32, name="fac_cols")

        own = sb.tile([P, SLOTS], F32, name="own")
        nc.vector.tensor_copy(own[:], a_sb[:].indirect(list1[:]))
        diff = sb.tile([P, SLOTS], F32, name="diff")
        nc.vector.tensor_tensor(diff[:], a_sb[:].indirect(list2[:]), own[:], ALU.subtract)
        for c in range(CHUNKS // 2):
            interleave_values(c)
            quantise_values(c)
        g_bf = sb.tile([P, Q, PACK], BF16, name="g_bf", align_bytes=64)
        interleave(nc.scalar.copy, g_bf[:], g_raw)
        g_code = sb.tile([P, Q], U32, name="g_code", align_bytes=64)
        g_scale = sb.tile([P, Q], U8, name="g_scale", align_bytes=64)
        quantise(g_code[:], g_scale[:], g_bf[:])
        nc.scalar.copy(out=share_row[:, SLOTS - LATE :], in_=share_col[:].to_broadcast([P, LATE]))
        nc.scalar.copy(out=fac_cols[:], in_=fac_ps[:, 0:BLOCKS])
        nc.vector.tensor_tensor(placed1[:].indirect(list1[:]), diff[:], share_row, ALU.mult)

        cf_turned = sb.tile([P, T], F32, name="cf_turned")
        cf = [bank("cf%d" % h, WEIGHED_BANK + h, HALF) for h in range(2)]

        def weigh(c):
            c_ps = bank("c_ps%d" % c, PRODUCT_BANK + c % 2, CHUNK)
            blocks = range(CHUNK_BLOCKS * c, CHUNK_BLOCKS * (c + 1))
            for block in blocks:
                nc.tensor.matmul_mx(
                    out=c_ps[:, span(block % CHUNK_BLOCKS, P)],
                    lhsT=v_code[:, span(block, P)].bitcast(FP8X4),
                    lhsT_scale=v_scale[:, span(block, P)],
                    rhs=g_code[:].bitcast(FP8X4),
                    rhs_scale=g_scale[:],
                    start=True,
                    stop=True,
                )
            for block in blocks:
                nc.scalar.activation(
                    out=cf_turned[:, span(block, P)],
                    in_=c_ps[:, span(block % CHUNK_BLOCKS, P)],
                    func=ACT.Copy,
                    scale=fac_cols[:, block : block + 1],
                )
            for block in blocks:
                turn(cf[block // BANK_BLOCKS][:, span(block % BANK_BLOCKS, P)], cf_turned[:, span(block, P)], True, True)

        last = CHUNKS - 1
        interleave_values(last - 1)
        quantise_values(last - 1)
        interleave_values(last)
        s = sb.tile([P, T], F32, name="s", tag="v_raw%d" % last)
        nc.vector.tensor_tensor(s[:], a_sb[:], placed1[:], ALU.add)
        quantise_values(last)
        neg_max = sb.tile([P, 1], F32, name="neg_max")
        nc.vector.tensor_reduce(out=neg_max[:], in_=s[:], axis=AXIS_X, op=ALU.max, negate=True)
        for c in range(CHUNKS):
            weigh(c)

        p = sb.tile([P, T], F32, name="p")
        z_half = sb.tile([P, 2], F32, name="z_half")
        w_half = sb.tile([P, 2], F32, name="w_half")
        for h in range(2):
            nc.scalar.activation(
                out=p[:, span(h, HALF)], in_=s[:, span(h, HALF)], func=ACT.Exp, bias=neg_max[:], accum_out=z_half[:, h : h + 1]
            )
        weighted = sb.tile([P, T], F32, name="weighted")
        z = sb.tile([P, 1], F32, name="z")
        inv_z = sb.tile([P, 1], F32, name="inv_z")

        def weighted_sum(h):
            cols = span(h, HALF)
            nc.vector.scalar_tensor_tensor(
                weighted[:, cols], cf[h][:], 1.0, p[:, cols], ALU.mult, ALU.mult, accum_out=w_half[:, h : h + 1]
            )

        weighted_sum(0)
        nc.vector.tensor_tensor(z[:], z_half[:, 0:1], z_half[:, 1:2], ALU.add)
        nc.vector.reciprocal(inv_z[:], z[:])
        weighted_sum(1)
        mean = sb.tile([P, 1], F32, name="mean")
        nc.vector.tensor_scalar(mean[:], w_half[:, 0:1], w_half[:, 1:2], inv_z[:], ALU.add, ALU.mult)
        prob = sb.tile([P, T], F32, name="prob")
        ds = sb.tile([P, T], F32, name="ds")
        for h in range(2):
            nc.scalar.activation(out=prob[:, span(h, HALF)], in_=p[:, span(h, HALF)], func=ACT.Copy, scale=inv_z[:])
            nc.vector.scalar_tensor_tensor(ds[:, span(h, HALF)], cf[h][:], mean[:], prob[:, span(h, HALF)], ALU.subtract, ALU.mult)

        ddl = sb.tile([P, SLOTS], F32, name="ddl")
        nc.vector.tensor_copy(ddl[:], ds[:].indirect(list1[:]))
        nc.vector.tensor_tensor(placed2[:].indirect(list2[:]), ddl[:], share_row, ALU.mult)
        nc.vector.tensor_tensor(placed1[:].indirect(list1[:]), ddl[:], neg_share_row[:], ALU.mult)

        old_turned = sb.tile([P, T], F32, name="old_turned")
        for h in range(2):
            stage = bank("old_stage%d" % h, WEIGHED_BANK + h, HALF)
            turn_half(stage, old_sb[:, span(h, HALF)], True, True)
            nc.scalar.copy(out=old_turned[:, span(h, HALF)], in_=stage[:])
        part = [bank("part%d" % h, SCORE_BANK + 2 + h, HALF) for h in range(2)]
        inner = [bank("inner%d" % h, SCORE_BANK + h, HALF) for h in range(2)]
        for h in range(2):
            turn_half(part[h], old_turned[:, span(h, HALF)], True, False)
        for h in range(2):
            turn_half(inner[h], ds[:, span(h, HALF)], True, False)
        inner_turned = sb.tile([P, T], F32, name="inner_turned")
        for h in range(2):
            turn_half(inner[h], placed2[:, span(h, HALF)], False, True)
            nc.scalar.activation(out=inner_turned[:, span(h, HALF)], in_=inner[h][:], func=ACT.Copy, scale=GAIN)
        for h in range(2):
            turn_half(part[h], inner_turned[:, span(h, HALF)], False, True)

        y = sb.tile([P, T], F32, name="y")
        for c in range(CHUNKS):
            cols = span(c, CHUNK)
            nc.vector.scalar_tensor_tensor(y[:, cols], placed1[:, cols], GAIN, part[c // 2][:, span(c % 2, CHUNK)], ALU.mult, ALU.add)
            queue = nc.sync if c % 2 == 0 else nc.scalar
            queue.dma_start(out=out[:, cols], in_=y[:, cols])
